import numpy as np
CORES = [3,11,19,27,35,43,51,59,67,75,83,91,131,139,147,155]
N = 16
ROOT = 14
def setup_inputs(rng):
    return {"x": rng.standard_normal((N, 128, 128), dtype=np.float32)}
def reference(x):
    y = np.full((N, 128, N * 128), np.nan, x.dtype)
    y[ROOT] = np.concatenate(list(x), axis=1)
    return {"y": y}

@@ -1,0 +1,96 @@
+W = 128
+ROOT_RANK = 14
+DIRECT = (0, 7)
+VIA_DIE0 = (7, 11)
+VIA_MATE = (11, 14)
+MATE_RELAYS = (2, 3, 6)
+
+SCRATCH = {
+    "stage": ("dram", [128, W], "float32"),
+    "hop": ("dram", [128, W], "float32"),
+    "land": ("sbuf", [128, 16 * W], "float32"),
+}
+SEMAPHORES = ["ld", "sent", "hoparr", "gdir", "gdie0", "gmate", "g15", "st_sync", "st_scal"]
+
+
+def _routes(cores):
+    root = cores[ROOT_RANK]
+    mate_base = ((root // 8) ^ 1) * 8
+    routes = {}
+    for j in range(*DIRECT):
+        routes[j] = (None, "gdir")
+    for j in range(*VIA_DIE0):
+        routes[j] = ((cores[j] // 8) * 8 + 7, "gdie0")
+    for k, j in enumerate(range(*VIA_MATE)):
+        routes[j] = (mate_base + MATE_RELAYS[k], "gmate")
+    routes[15] = (None, "g15")
+    return routes
+
+
+def _engines(mask):
+    return bin(mask).count("1")
+
+
+def rank_program(g, core, T, topo):
+    cores = list(T.cores)
+    root = cores[ROOT_RANK]
+    routes = _routes(cores)
+    sem = T.sem
+
+    if core == root:
+        _root_program(g, T, topo, cores, routes)
+        return
+
+    sent = [0]
+
+    def write(dst, out_ap, in_ap, remote_sem):
+        rid, pid = topo.addr(dst, core)
+        mask = topo.mask(core, dst)
+        g.remote_dma(out_ap=out_ap, in_ap=in_ap, remote_sem=remote_sem, local_sem=sem.sent,
+                     pid=pid, routing_id=rid, dma_engine_mask=mask)
+        sent[0] += _engines(mask)
+
+    rank = T.rank_of(core)
+    if rank is not None:
+        g.sync.dma_start(T.stage[:], T.x[:]).then_inc(sem.ld, 16)
+        g.wait_ge(sem.ld, 16)
+        helper, grp = routes[rank]
+        if helper is None:
+            write(root, T.land[:, rank * W:(rank + 1) * W], T.stage[:], sem[grp])
+        else:
+            write(helper, T.hop[:], T.stage[:], sem.hoparr)
+
+    for j in sorted(routes):
+        helper, grp = routes[j]
+        if helper == core:
+            g.wait_ge(sem.hoparr, _engines(topo.mask(cores[j], core)))
+            write(root, T.land[:, j * W:(j + 1) * W], T.hop[:], sem[grp])
+
+    if sent[0]:
+        g.wait_ge(sem.sent, sent[0])
+
+
+def _root_program(g, T, topo, cores, routes):
+    sem = T.sem
+    root = cores[ROOT_RANK]
+
+    def total(name):
+        n = 0
+        for j in routes:
+            helper, grp = routes[j]
+            if grp == name:
+                last = cores[j] if helper is None else helper
+                n += _engines(topo.mask(last, root))
+        return n
+
+    def store(q, lo, hi, name, done):
+        q.wait_ge(sem[name], total(name))
+        q.dma_start(T.y[:, lo * W:hi * W], T.land[:, lo * W:hi * W]).then_inc(done, 16)
+
+    g.scalar.dma_start(T.y[:, ROOT_RANK * W:(ROOT_RANK + 1) * W], T.x[:]).then_inc(sem.st_scal, 16)
+    store(g.sync, 15, 16, "g15", sem.st_sync)
+    store(g.sync, DIRECT[0], DIRECT[1], "gdir", sem.st_sync)
+    store(g.scalar, VIA_DIE0[0], VIA_DIE0[1], "gdie0", sem.st_scal)
+    store(g.scalar, VIA_MATE[0], VIA_MATE[1], "gmate", sem.st_scal)
+    g.wait_ge(sem.st_sync, 32)
+    g.wait_ge(sem.st_scal, 48)

@@ -1,16 +1,17 @@
 W = 128
 ROOT_RANK = 14
-DIRECT = (0, 7)
+DIRECT = (0, 4)
+SECOND = (4, 7)
 VIA_DIE0 = (7, 11)
 VIA_MATE = (11, 14)
-MATE_RELAYS = (2, 3, 6)
+MATE_RELAYS = (2, 3, 6, 7)
 
 SCRATCH = {
     "stage": ("dram", [128, W], "float32"),
     "hop": ("dram", [128, W], "float32"),
     "land": ("sbuf", [128, 16 * W], "float32"),
 }
-SEMAPHORES = ["ld", "sent", "hoparr", "gdir", "gdie0", "gmate", "g15", "st_sync", "st_scal"]
+SEMAPHORES = ["ld", "sent", "hoparr", "gdir", "gsec", "gdie0", "gmate", "g15", "st_sync", "st_scal"]
 
 
 def _routes(cores):
@@ -19,6 +20,8 @@ def _routes(cores):
     routes = {}
     for j in range(*DIRECT):
         routes[j] = (None, "gdir")
+    for j in range(*SECOND):
+        routes[j] = ((cores[j] // 8) * 8 + 2, "gsec")
     for j in range(*VIA_DIE0):
         routes[j] = ((cores[j] // 8) * 8 + 7, "gdie0")
     for k, j in enumerate(range(*VIA_MATE)):
@@ -90,7 +93,8 @@ def _root_program(g, T, topo, cores, routes):
     g.scalar.dma_start(T.y[:, ROOT_RANK * W:(ROOT_RANK + 1) * W], T.x[:]).then_inc(sem.st_scal, 16)
     store(g.sync, 15, 16, "g15", sem.st_sync)
     store(g.sync, DIRECT[0], DIRECT[1], "gdir", sem.st_sync)
+    store(g.sync, SECOND[0], SECOND[1], "gsec", sem.st_sync)
     store(g.scalar, VIA_DIE0[0], VIA_DIE0[1], "gdie0", sem.st_scal)
     store(g.scalar, VIA_MATE[0], VIA_MATE[1], "gmate", sem.st_scal)
-    g.wait_ge(sem.st_sync, 32)
+    g.wait_ge(sem.st_sync, 48)
     g.wait_ge(sem.st_scal, 48)

W = 128
ROOT_RANK = 14
DIRECT = (0, 4)
SECOND = (4, 7)
VIA_DIE0 = (7, 11)
VIA_MATE = (11, 14)
MATE_RELAYS = (2, 3, 6, 7)

SCRATCH = {
    "stage": ("dram", [128, W], "float32"),
    "hop": ("dram", [128, W], "float32"),
    "land": ("sbuf", [128, 16 * W], "float32"),
}
SEMAPHORES = ["ld", "sent", "hoparr", "gdir", "gsec", "gdie0", "gmate", "g15", "st_sync", "st_scal"]


def _routes(cores):
    root = cores[ROOT_RANK]
    mate_base = ((root // 8) ^ 1) * 8
    routes = {}
    for j in range(*DIRECT):
        routes[j] = (None, "gdir")
    for j in range(*SECOND):
        routes[j] = ((cores[j] // 8) * 8 + 2, "gsec")
    for j in range(*VIA_DIE0):
        routes[j] = ((cores[j] // 8) * 8 + 7, "gdie0")
    for k, j in enumerate(range(*VIA_MATE)):
        routes[j] = (mate_base + MATE_RELAYS[k], "gmate")
    routes[15] = (None, "g15")
    return routes


def _engines(mask):
    return bin(mask).count("1")


def rank_program(g, core, T, topo):
    cores = list(T.cores)
    root = cores[ROOT_RANK]
    routes = _routes(cores)
    sem = T.sem

    if core == root:
        _root_program(g, T, topo, cores, routes)
        return

    sent = [0]

    def write(dst, out_ap, in_ap, remote_sem):
        rid, pid = topo.addr(dst, core)
        mask = topo.mask(core, dst)
        g.remote_dma(out_ap=out_ap, in_ap=in_ap, remote_sem=remote_sem, local_sem=sem.sent,
                     pid=pid, routing_id=rid, dma_engine_mask=mask)
        sent[0] += _engines(mask)

    rank = T.rank_of(core)
    if rank is not None:
        g.sync.dma_start(T.stage[:], T.x[:]).then_inc(sem.ld, 16)
        g.wait_ge(sem.ld, 16)
        helper, grp = routes[rank]
        if helper is None:
            write(root, T.land[:, rank * W:(rank + 1) * W], T.stage[:], sem[grp])
        else:
            write(helper, T.hop[:], T.stage[:], sem.hoparr)

    for j in sorted(routes):
        helper, grp = routes[j]
        if helper == core:
            g.wait_ge(sem.hoparr, _engines(topo.mask(cores[j], core)))
            write(root, T.land[:, j * W:(j + 1) * W], T.hop[:], sem[grp])

    if sent[0]:
        g.wait_ge(sem.sent, sent[0])


def _root_program(g, T, topo, cores, routes):
    sem = T.sem
    root = cores[ROOT_RANK]

    def total(name):
        n = 0
        for j in routes:
            helper, grp = routes[j]
            if grp == name:
                last = cores[j] if helper is None else helper
                n += _engines(topo.mask(last, root))
        return n

    def store(q, lo, hi, name, done):
        q.wait_ge(sem[name], total(name))
        q.dma_start(T.y[:, lo * W:hi * W], T.land[:, lo * W:hi * W]).then_inc(done, 16)

    g.scalar.dma_start(T.y[:, ROOT_RANK * W:(ROOT_RANK + 1) * W], T.x[:]).then_inc(sem.st_scal, 16)
    store(g.sync, 15, 16, "g15", sem.st_sync)
    store(g.sync, DIRECT[0], DIRECT[1], "gdir", sem.st_sync)
    store(g.sync, SECOND[0], SECOND[1], "gsec", sem.st_sync)
    store(g.scalar, VIA_DIE0[0], VIA_DIE0[1], "gdie0", sem.st_scal)
    store(g.scalar, VIA_MATE[0], VIA_MATE[1], "gmate", sem.st_scal)
    g.wait_ge(sem.st_sync, 48)
    g.wait_ge(sem.st_scal, 48)
